import numpy as np
import ml_dtypes


def mxq(x, axis, fmt="e4m3"):
    dtype, down = {"e4m3": (ml_dtypes.float8_e4m3fn, 7), "e5m2": (ml_dtypes.float8_e5m2, 14)}[fmt]
    v = np.moveaxis(np.asarray(x, np.float32).astype(ml_dtypes.bfloat16).astype(np.float64), axis, -1)
    blocks = v.reshape(v.shape[:-1] + (-1, 32))
    amax = np.abs(blocks).max(-1, keepdims=True)
    byte = np.maximum(np.where(amax > 0, np.frexp(amax)[1] - 1 + 127, 0) - down, 1)
    scale = np.exp2(byte - 127.0)
    codes = (blocks / scale).astype(np.float32).astype(dtype).astype(np.float64)
    return np.moveaxis((codes * scale).reshape(v.shape), -1, axis)


WIDE = False


def mx_kscale(k):
    if not WIDE:
        return np.ones(k)
    levels = np.array([10, -10, 5, -5, 0])
    if k % 512:
        return np.exp2(np.random.permutation(np.resize(levels, k // 32))).repeat(32)
    a = np.empty((k // 512, 16))
    for p in range(k // 512):
        a[p, :8] = np.random.permutation(np.resize(levels, 8))
        for g in range(8):
            far = levels[np.abs(levels - a[p, g]) >= 10]
            a[p, g + 8] = far[np.random.randint(len(far))]
    return np.exp2(a.ravel()).repeat(32)


BF16 = ml_dtypes.bfloat16


def bf(x):
    return np.asarray(x, np.float32).astype(BF16)


def f64(x):
    return np.asarray(x).astype(np.float64)


E2M1 = np.array([0.0, 0.5, 1.0, 1.5, 2.0, 3.0, 4.0, 6.0, -0.0, -0.5, -1.0, -1.5, -2.0, -3.0, -4.0, -6.0])


def pack_weight(w, fmt):
    k, n = w.shape
    w = f64(bf(w)).reshape(k // 32, 32, n)
    amax = np.abs(w).max(1)
    if fmt == "e4m3":
        byte = np.frexp(amax)[1] - 1 + 127 - 7
    else:
        mant, ex = np.frexp(amax / 6.0)
        byte = np.where(mant > 0.5, ex, ex - 1) + 127
    byte = np.clip(np.where(amax > 0, byte, 1), 1, 254)
    scaled = (w * np.exp2(127.0 - byte)[:, None, :]).reshape(k, n).astype(np.float32)
    by_word = np.ascontiguousarray(scaled.reshape(k // 512, 128, 4, n).transpose(0, 1, 3, 2))
    if fmt == "e4m3":
        words = by_word.astype(ml_dtypes.float8_e4m3fn).view(np.uint8)
    else:
        c = by_word.astype(ml_dtypes.float4_e2m1fn).view(np.uint8) & 0xF
        words = c[..., 0::2] | (c[..., 1::2] << 4)
    return np.ascontiguousarray(words), np.ascontiguousarray(byte.astype(np.uint8).reshape(k // 512, 16, n))


def unpack_weight(words, scales, fmt):
    g, p, n, _ = words.shape
    if fmt == "e4m3":
        vals = np.ascontiguousarray(words).view(ml_dtypes.float8_e4m3fn).astype(np.float64)
    else:
        nib = np.empty((g, p, n, 4), np.uint8)
        nib[..., 0::2] = words & 0xF
        nib[..., 1::2] = words >> 4
        vals = E2M1[nib]
    vals = vals * np.repeat(np.exp2(scales.astype(np.float64) - 127.0), 8, axis=1)[..., None]
    return vals.transpose(0, 1, 3, 2).reshape(g * 512, n)
def pack4(w):
    words, scales = pack_weight(w, "e2m1")
    return words.reshape(words.shape[0], 128, -1), scales


def unpack4(words, scales):
    return unpack_weight(words.reshape(words.shape[0], 128, -1, 2), scales, "e2m1")


M, K, N, A, L = 1024, 1024, 1024, 32, 256


def setup_inputs():
    s = mx_kscale(K)
    a = np.random.permutation(L)[:A]
    b = np.random.permutation(L)[:A]
    lag = np.abs(a[:, None] - b[None, :]).reshape(K)
    mean = 1.0 / np.bincount(lag, minlength=L)[lag]
    hann = mean * (0.5 + 0.5 * np.cos(np.pi * lag / L))
    mean = mean / np.sqrt(np.mean(mean ** 2))
    hann = hann / np.sqrt(np.mean(hann ** 2))
    wave = np.cos(np.pi * lag[:, None] * np.arange(N) / N) * np.sqrt(2.0 / K)
    w1 = wave * mean[:, None] * (1 + 0.1 * np.random.standard_normal((K, N)))
    w2 = wave * hann[:, None] * (1 + 0.1 * np.random.standard_normal((K, N)))
    w1_words, w1_scales = pack4(w1 / s[:, None])
    w2_words, w2_scales = pack_weight(w2 / s[:, None], "e4m3")
    return {"x": bf(np.random.standard_normal((M, K)) * s),
            "w1_words": w1_words, "w1_scales": w1_scales,
            "w2_words": w2_words, "w2_scales": w2_scales,
            "w3": bf(np.random.standard_normal((K, N)) / np.sqrt(K) / s[:, None])}


def reference(x, w1_words, w1_scales, w2_words, w2_scales, w3):
    xq = mxq(f64(x), 1, "e4m3")
    p1 = xq @ unpack4(w1_words, w1_scales)
    p2 = xq @ unpack_weight(w2_words, w2_scales, "e4m3")
    p3 = xq @ mxq(f64(w3), 0, "e4m3")
    return np.minimum(np.abs(p1), np.abs(p2)) + p3

@@ -1,0 +1,204 @@
+from contextlib import ExitStack
+import concourse.mybir as mybir
+from concourse.masks import make_identity
+
+FLOPS = 3 * 2 * 1024 * 1024 * 1024
+
+F32 = mybir.dt.float32
+BF16 = mybir.dt.bfloat16
+U32 = mybir.dt.uint32
+I32 = mybir.dt.int32
+U8 = mybir.dt.uint8
+FP8X4 = mybir.dt.float8_e4m3fn_x4
+FP4X4 = mybir.dt.float4_e2m1fn_x4
+ABS = mybir.ActivationFunctionType.Abs
+ALU = mybir.AluOpType
+P = 128
+
+ORDER = """LX_0 LX_1 LS1 L1_a LX_23 L3_g0 LX_45 LS2 L2_a L3_g1 LX_67 T_0 T_1 XC_0_S XC_1_S XQ_0 XQ_1 P_1_0_0 P_1_0_1 A_1_0_0 A_1_0_1 T_2 T_3 XC_2_S P_1_1_0 XC_3_S XQ_2 P_1_1_1 A_1_1_0 XQ_3 WC_0_0_V P_1_2_0 A_1_1_1 P_1_2_1 A_1_2_0 T_4 WC_0_1_V A_1_2_1 T_5 XC_4_S P_1_3_0 XC_5_S XQ_4 WQ_0_0 P_1_3_1 A_1_3_0 P_1_4_0 XQ_5 A_1_3_1 WQ_0_1 P_1_4_1 A_1_4_0 P_2_0_0 A_1_4_1 P_2_0_1 WC_1_0_V A_2_0_0 P_2_1_0 A_2_0_1 P_2_1_1 A_2_1_0 M_0_0 T_6 A_2_1_1 WQ_1_0 T_7 XC_6_S M_0_1 P_1_5_0 XC_7_S M_1_0 P_1_5_1 A_1_5_0 XQ_6 P_2_2_0 WC_1_1_V A_1_5_1 P_2_2_1 A_2_2_0 P_2_3_0 A_2_2_1 M_1_1 P_2_3_1 A_2_3_0 WQ_1_1 P_2_4_0 A_2_3_1 M_2_0 P_2_4_1 A_2_4_0 M_2_1 P_3_0_0 A_2_4_1 XQ_7 P_3_0_1 O_0_0 P_3_1_0 O_0_1 P_3_1_1 O_1_0 P_2_5_0 O_1_1 P_2_5_1 A_2_5_0 M_3_0 P_1_6_0 A_2_5_1 M_3_1 P_1_6_1 A_1_6_0 M_4_0 P_3_2_0 A_1_6_1 M_4_1 P_3_2_1 O_2_0 P_2_6_0 O_2_1 P_2_6_1 A_2_6_0 M_5_0 P_3_3_0 A_2_6_1 M_5_1 P_3_3_1 O_3_0 P_1_7_0 O_3_1 P_1_7_1 A_1_7_0 M_6_0 P_2_7_0 A_1_7_1 M_6_1 P_2_7_1 A_2_7_0 P_3_4_0 A_2_7_1 M_7_0 P_3_4_1 O_4_0 P_3_5_0 O_4_1 P_3_5_1 O_5_0 P_3_6_0 O_5_1 P_3_6_1 O_6_0 P_3_7_0 O_6_1 P_3_7_1 M_7_1 O_7_0 O_7_1"""
+
+
+def tile_coarray_cosine_spectrum_s10_kernel(tc, x, w1_words, w1_scales, w2_words, w2_scales, w3, out):
+    nc = tc.nc
+    with ExitStack() as ctx:
+        one = ctx.enter_context(tc.tile_pool(name="one", bufs=1))
+        tiles = ctx.enter_context(tc.tile_pool(name="tiles", bufs=8))
+        psum = ctx.enter_context(tc.psum_pool(name="psum", bufs=6))
+        psum_t = ctx.enter_context(tc.psum_pool(name="psum_t", bufs=2))
+
+        ident = one.tile([P, P], F32, name="ident")
+        w1 = one.tile([P, 2, 2048], U8, name="w1", align_bytes=64)
+        s1 = one.tile([P, 2, 1024], U8, name="s1", align_bytes=64)
+        w2 = one.tile([P, 2, 4096], U8, name="w2", align_bytes=64)
+        s2 = one.tile([P, 2, 1024], U8, name="s2", align_bytes=64)
+        raw3 = [one.tile([P, 4, 1024], BF16, name="raw3_%d" % g, align_bytes=64) for g in range(2)]
+        grp3 = [one.tile([P, 2048], BF16, name="grp3_%d" % i, align_bytes=64) for i in range(4)]
+        w3c = [one.tile([P, 512], U32, name="w3c_%d" % i, align_bytes=64) for i in range(4)]
+        w3s = [one.tile([P, 512], U8, name="w3s_%d" % i, align_bytes=64) for i in range(4)]
+        dummy = one.tile([P, 1], F32, name="dummy")
+        wbf = one.tile([P, 512], BF16, name="wbf", align_bytes=64)
+        wcd = one.tile([P, 128], U32, name="wcd", align_bytes=64)
+        wsc = one.tile([P, 128], U8, name="wsc", align_bytes=64)
+
+        xr = [None] * 8
+        xt = [None] * 8
+        xg = [None] * 8
+        xc = [None] * 8
+        xs = [None] * 8
+        a = {}
+        ot = {}
+        ps = {}
+
+        def load_x(ms):
+            if len(ms) == 1:
+                t = tiles.tile([P, 1, 1024], BF16, name="xr1", align_bytes=64, bufs=2)
+            else:
+                t = tiles.tile([P, 2, 1024], BF16, name="xr2", align_bytes=64, bufs=3)
+            for i in range(len(ms)):
+                xr[ms[i]] = t[:, i, :]
+            m = ms[0]
+            nc.sync.dma_start(out=t[:], in_=x[128 * m : 128 * (m + len(ms)), :].rearrange("(i r) k -> r i k", r=128))
+
+        def load_scales(s, src):
+            for q in range(4):
+                nc.sync.dma_start(
+                    out=s[32 * q : 32 * q + 4, :, :].bitcast(I32),
+                    in_=src[:, 4 * q : 4 * q + 4, :].rearrange("g q n -> q g n").bitcast(I32),
+                )
+
+        def load_w1(h):
+            sl = slice(0, 2048) if h == "a" else slice(1024 * int(h), 1024 * (int(h) + 1))
+            nc.sync.dma_start(out=w1[:, :, sl].bitcast(I32), in_=w1_words[:, :, sl].rearrange("g p b -> p g b").bitcast(I32))
+
+        def load_w2(h):
+            a0, a1 = (0, 1024) if h == "a" else (512 * int(h), 512 * (int(h) + 1))
+            nc.sync.dma_start(
+                out=w2[:, :, 4 * a0 : 4 * a1].bitcast(I32),
+                in_=w2_words[:, :, a0:a1, :].rearrange("g p n t -> p g (n t)").bitcast(I32),
+            )
+
+        def load_w3(s):
+            if s[0] == "g":
+                g, sl = int(s[1]), slice(0, 1024)
+            else:
+                g, h = int(s[0]), int(s[1])
+                sl = slice(512 * h, 512 * (h + 1))
+            nc.sync.dma_start(out=raw3[g][:, :, sl], in_=w3[512 * g : 512 * (g + 1), sl].rearrange("(p j) n -> p j n", j=4))
+
+        def transp(m):
+            xt[m] = psum_t.tile([P, 2, 2, 128], F32, name="xt")
+            words = xr[m].bitcast(F32)
+            for g in range(2):
+                for u in range(2):
+                    nc.tensor.transpose(xt[m][:, g, u, :], words[:, 256 * g + u : 256 * (g + 1) : 2], ident[:])
+
+        def xcopy(m, eng):
+            xg[m] = tiles.tile([P, 1024], BF16, name="xg", align_bytes=64)
+            o = xg[m][:].bitcast(F32).rearrange("p (g r u) -> p g r u", g=2, u=2)
+            i = xt[m][:].rearrange("p g u r -> p g r u")
+            if eng == "S":
+                nc.scalar.copy(out=o, in_=i)
+            else:
+                nc.vector.tensor_copy(out=o, in_=i)
+
+        def xquant(m):
+            xc[m] = tiles.tile([P, 256], U32, name="xc", align_bytes=64)
+            xs[m] = tiles.tile([P, 256], U8, name="xs", align_bytes=64)
+            nc.vector.quantize_mx(out=xc[m][:].bitcast(FP8X4), scales=xs[m][:], in_=xg[m][:])
+
+        def w3copy(g, h, eng):
+            o = grp3[2 * g + h][:].rearrange("p (c i t) -> p c t i", i=4, t=4)
+            i = raw3[g][:, :, 512 * h : 512 * (h + 1)].rearrange("p t (c i) -> p c t i", i=4)
+            if eng == "S":
+                nc.scalar.copy(out=o, in_=i)
+            else:
+                nc.vector.tensor_copy(out=o, in_=i)
+
+        def w3quant(g, h):
+            k = 2 * g + h
+            nc.vector.quantize_mx(out=w3c[k][:].bitcast(FP8X4), scales=w3s[k][:], in_=grp3[k][:])
+
+        def product(n, m, h):
+            acc = psum.tile([P, 512], F32, name="acc")
+            ps[(n, m, h)] = acc
+            for g in range(2):
+                if n == 1:
+                    rhs = w1[:, g, 1024 * h : 1024 * (h + 1)].bitcast(FP4X4)
+                    rsc = s1[:, g, 512 * h : 512 * (h + 1)]
+                elif n == 2:
+                    rhs = w2[:, g, 2048 * h : 2048 * (h + 1)].bitcast(FP8X4)
+                    rsc = s2[:, g, 512 * h : 512 * (h + 1)]
+                else:
+                    rhs = w3c[2 * g + h][:].bitcast(FP8X4)
+                    rsc = w3s[2 * g + h][:]
+                nc.tensor.matmul_mx(
+                    out=acc[:],
+                    lhsT=xc[m][:, 128 * g : 128 * (g + 1)].bitcast(FP8X4),
+                    lhsT_scale=xs[m][:, 128 * g : 128 * (g + 1)],
+                    rhs=rhs,
+                    rhs_scale=rsc,
+                    start=(g == 0),
+                    stop=(g == 1),
+                )
+
+        def absolute(n, m, h):
+            if (n, m) not in a:
+                a[(n, m)] = tiles.tile([P, 1024], F32, name="a%d" % n)
+            nc.scalar.activation(out=a[(n, m)][:, 512 * h : 512 * (h + 1)], in_=ps[(n, m, h)][:], func=ABS)
+
+        def minimum(m, h):
+            sl = slice(512 * h, 512 * (h + 1))
+            nc.vector.tensor_tensor(out=a[(1, m)][:, sl], in0=a[(1, m)][:, sl], in1=a[(2, m)][:, sl], op=ALU.min)
+
+        def finish(m, h):
+            if m not in ot:
+                ot[m] = tiles.tile([P, 1024], F32, name="ot")
+            sl = slice(512 * h, 512 * (h + 1))
+            nc.vector.tensor_tensor(out=ot[m][:, sl], in0=ps[(3, m, h)][:], in1=a[(1, m)][:, sl], op=ALU.add)
+            nc.sync.dma_start(out=out[128 * m : 128 * (m + 1), sl], in_=ot[m][:, sl])
+
+        with tc.manual_schedule():
+            nc.vector.memset(wbf[:], 1.0)
+            nc.vector.quantize_mx(out=wcd[:].bitcast(FP8X4), scales=wsc[:], in_=wbf[:])
+            nc.vector.memset(s1[:].rearrange("p g n -> p (g n)").bitcast(I32), 0)
+            nc.vector.memset(s2[:].rearrange("p g n -> p (g n)").bitcast(I32), 0)
+            nc.vector.memset(dummy[:], 0.0)
+            nc.scalar.activation(out=dummy[:], in_=dummy[:], func=ABS)
+            make_identity(nc, ident[:])
+            warm = psum.tile([P, 512], F32, name="acc")
+            for i in range(12):
+                nc.tensor.matmul_mx(out=warm[:, 0:128], lhsT=wcd[:].bitcast(FP8X4), lhsT_scale=wsc[:], rhs=wcd[:].bitcast(FP8X4), rhs_scale=wsc[:], start=True, stop=True)
+            for step in ORDER.split():
+                w = step.split("_")
+                k = w[0]
+                v = [int(c) for c in w[1:] if c in "01234567"]
+                if k == "LX":
+                    load_x([int(c) for c in w[1]])
+                elif k == "LS1":
+                    load_scales(s1, w1_scales)
+                elif k == "LS2":
+                    load_scales(s2, w2_scales)
+                elif k == "L1":
+                    load_w1(w[1])
+                elif k == "L2":
+                    load_w2(w[1])
+                elif k == "L3":
+                    load_w3(w[1])
+                elif k == "T":
+                    transp(v[0])
+                elif k == "XC":
+                    xcopy(v[0], w[2])
+                elif k == "XQ":
+                    xquant(v[0])
+                elif k == "WC":
+                    w3copy(v[0], v[1], w[3])
+                elif k == "WQ":
+                    w3quant(v[0], v[1])
+                elif k == "P":
+                    product(v[0], v[1], v[2])
+                elif k == "A":
+                    absolute(v[0], v[1], v[2])
+                elif k == "M":
+                    minimum(v[0], v[1])
+                elif k == "O":
+                    finish(v[0], v[1])

@@ -15,7 +15,7 @@ ABS = mybir.ActivationFunctionType.Abs
 ALU = mybir.AluOpType
 P = 128
 
-ORDER = """LX_0 LX_1 LS1 L1_a LX_23 L3_g0 LX_45 LS2 L2_a L3_g1 LX_67 T_0 T_1 XC_0_S XC_1_S XQ_0 XQ_1 P_1_0_0 P_1_0_1 A_1_0_0 A_1_0_1 T_2 T_3 XC_2_S P_1_1_0 XC_3_S XQ_2 P_1_1_1 A_1_1_0 XQ_3 WC_0_0_V P_1_2_0 A_1_1_1 P_1_2_1 A_1_2_0 T_4 WC_0_1_V A_1_2_1 T_5 XC_4_S P_1_3_0 XC_5_S XQ_4 WQ_0_0 P_1_3_1 A_1_3_0 P_1_4_0 XQ_5 A_1_3_1 WQ_0_1 P_1_4_1 A_1_4_0 P_2_0_0 A_1_4_1 P_2_0_1 WC_1_0_V A_2_0_0 P_2_1_0 A_2_0_1 P_2_1_1 A_2_1_0 M_0_0 T_6 A_2_1_1 WQ_1_0 T_7 XC_6_S M_0_1 P_1_5_0 XC_7_S M_1_0 P_1_5_1 A_1_5_0 XQ_6 P_2_2_0 WC_1_1_V A_1_5_1 P_2_2_1 A_2_2_0 P_2_3_0 A_2_2_1 M_1_1 P_2_3_1 A_2_3_0 WQ_1_1 P_2_4_0 A_2_3_1 M_2_0 P_2_4_1 A_2_4_0 M_2_1 P_3_0_0 A_2_4_1 XQ_7 P_3_0_1 O_0_0 P_3_1_0 O_0_1 P_3_1_1 O_1_0 P_2_5_0 O_1_1 P_2_5_1 A_2_5_0 M_3_0 P_1_6_0 A_2_5_1 M_3_1 P_1_6_1 A_1_6_0 M_4_0 P_3_2_0 A_1_6_1 M_4_1 P_3_2_1 O_2_0 P_2_6_0 O_2_1 P_2_6_1 A_2_6_0 M_5_0 P_3_3_0 A_2_6_1 M_5_1 P_3_3_1 O_3_0 P_1_7_0 O_3_1 P_1_7_1 A_1_7_0 M_6_0 P_2_7_0 A_1_7_1 M_6_1 P_2_7_1 A_2_7_0 P_3_4_0 A_2_7_1 M_7_0 P_3_4_1 O_4_0 P_3_5_0 O_4_1 P_3_5_1 O_5_0 P_3_6_0 O_5_1 P_3_6_1 O_6_0 P_3_7_0 O_6_1 P_3_7_1 M_7_1 O_7_0 O_7_1"""
+ORDER = """LX_0 LX_1 LS1 L1_a LX_23 L3_g0 LX_45 LS2 L2_a L3_g1 LX_67 T_0 T_1 XC_0_S XC_1_S XQ_0 P_1_0_0 XQ_1 P_1_0_1 A_1_0_0 A_1_0_1 T_2 T_3 XC_2_S P_1_1_0 XC_3_S XQ_2 P_1_1_1 A_1_1_0 XQ_3 WC_0_0_V P_1_2_0 A_1_1_1 P_1_2_1 A_1_2_0 WC_0_1_V T_4 A_1_2_1 T_5 XC_4_S P_1_3_0 XC_5_S XQ_4 WQ_0_0 P_1_3_1 A_1_3_0 XQ_5 P_1_4_0 A_1_3_1 WQ_0_1 P_1_4_1 A_1_4_0 P_2_0_0 A_1_4_1 WC_1_0_V P_2_0_1 A_2_0_0 P_2_1_0 A_2_0_1 P_2_1_1 A_2_1_0 WC_1_1_V T_6 A_2_1_1 T_7 XC_6_S WQ_1_0 P_1_5_0 XC_7_S WQ_1_1 P_1_5_1 A_1_5_0 M_0_f P_2_2_0 A_1_5_1 P_2_2_1 A_2_2_0 XQ_6 P_2_3_0 M_1_f A_2_2_1 P_2_3_1 A_2_3_0 M_2_f P_2_4_0 A_2_3_1 P_2_4_1 A_2_4_0 XQ_7 P_3_0_0 A_2_4_1 M_3_f P_3_0_1 P_2_5_0 O_0_0 P_2_5_1 A_2_5_0 O_0_1 P_3_1_0 A_2_5_1 M_4_f P_3_1_1 P_1_6_0 O_1_0 P_1_6_1 A_1_6_0 O_1_1 P_3_2_0 A_1_6_1 M_5_f P_3_2_1 P_2_6_0 O_2_0 P_2_6_1 A_2_6_0 O_2_1 P_3_3_0 A_2_6_1 P_3_3_1 O_3_0 P_1_7_0 O_3_1 P_1_7_1 A_1_7_0 M_6_f P_3_4_0 A_1_7_1 P_3_4_1 O_4_0 P_3_5_0 O_4_1 P_3_5_1 O_5_0 P_2_7_0 O_5_1 P_2_7_1 A_2_7_0 P_3_6_0 A_2_7_1 M_7_0 P_3_6_1 O_6_0 P_3_7_0 O_6_1 P_3_7_1 M_7_1 O_7_0 O_7_1"""
 
 
 def tile_coarray_cosine_spectrum_s10_kernel(tc, x, w1_words, w1_scales, w2_words, w2_scales, w3, out):
@@ -46,8 +46,15 @@ def tile_coarray_cosine_spectrum_s10_kernel(tc, x, w1_words, w1_scales, w2_words
         xc = [None] * 8
         xs = [None] * 8
         a = {}
+        xo = {}
+        pc = {}
         ot = {}
         ps = {}
+
+        def warm_up(n):
+            warm = psum.tile([P, 512], F32, name="acc")
+            for i in range(n):
+                nc.tensor.matmul_mx(out=warm[:, 0:128], lhsT=wcd[:].bitcast(FP8X4), lhsT_scale=wsc[:], rhs=wcd[:].bitcast(FP8X4), rhs_scale=wsc[:], start=True, stop=True)
 
         def load_x(ms):
             if len(ms) == 1:
@@ -59,9 +66,9 @@ def tile_coarray_cosine_spectrum_s10_kernel(tc, x, w1_words, w1_scales, w2_words
             m = ms[0]
             nc.sync.dma_start(out=t[:], in_=x[128 * m : 128 * (m + len(ms)), :].rearrange("(i r) k -> r i k", r=128))
 
-        def load_scales(s, src):
+        def load_scales(s, src, eng=nc.sync):
             for q in range(4):
-                nc.sync.dma_start(
+                eng.dma_start(
                     out=s[32 * q : 32 * q + 4, :, :].bitcast(I32),
                     in_=src[:, 4 * q : 4 * q + 4, :].rearrange("g q n -> q g n").bitcast(I32),
                 )
@@ -87,10 +94,23 @@ def tile_coarray_cosine_spectrum_s10_kernel(tc, x, w1_words, w1_scales, w2_words
 
         def transp(m):
             xt[m] = psum_t.tile([P, 2, 2, 128], F32, name="xt")
-            words = xr[m].bitcast(F32)
             for g in range(2):
                 for u in range(2):
-                    nc.tensor.transpose(xt[m][:, g, u, :], words[:, 256 * g + u : 256 * (g + 1) : 2], ident[:])
+                    if m in xo:
+                        src = xo[m][:, 256 * g + 128 * u : 256 * g + 128 * (u + 1)]
+                    else:
+                        src = xr[m].bitcast(F32)[:, 256 * g + u : 256 * (g + 1) : 2]
+                    nc.tensor.transpose(xt[m][:, g, u, :], src, ident[:])
+
+        def reorder(m, eng):
+            t = tiles.tile([P, 512], F32, name="xo", align_bytes=64)
+            o = t[:].rearrange("p (g u w) -> p g u w", g=2, u=2)
+            i = xr[m].bitcast(F32).rearrange("p (g w u) -> p g u w", g=2, u=2)
+            if eng == "S":
+                nc.scalar.copy(out=o, in_=i)
+            else:
+                nc.vector.tensor_copy(out=o, in_=i)
+            xo[m] = t
 
         def xcopy(m, eng):
             xg[m] = tiles.tile([P, 1024], BF16, name="xg", align_bytes=64)
@@ -147,37 +167,49 @@ def tile_coarray_cosine_spectrum_s10_kernel(tc, x, w1_words, w1_scales, w2_words
             nc.scalar.activation(out=a[(n, m)][:, 512 * h : 512 * (h + 1)], in_=ps[(n, m, h)][:], func=ABS)
 
         def minimum(m, h):
-            sl = slice(512 * h, 512 * (h + 1))
+            sl = slice(0, 1024) if h == "f" else slice(512 * int(h), 512 * (int(h) + 1))
             nc.vector.tensor_tensor(out=a[(1, m)][:, sl], in0=a[(1, m)][:, sl], in1=a[(2, m)][:, sl], op=ALU.min)
+
+        def copy_g(m, h):
+            pc[(m, h)] = tiles.tile([P, 512], F32, name="pc", bufs=4)
+            nc.scalar.copy(out=pc[(m, h)][:], in_=ps[(3, m, h)][:])
+
+        def finish_g(m, h):
+            if m not in ot:
+                ot[m] = tiles.tile([P, 1024], F32, name="ot")
+            sl = slice(512 * h, 512 * (h + 1))
+            nc.gpsimd.tensor_tensor(out=ot[m][:, sl], in0=pc[(m, h)][:], in1=a[(1, m)][:, sl], op=ALU.add)
+            nc.sync.dma_start(out=out[128 * m : 128 * (m + 1), sl], in_=ot[m][:, sl])
 
         def finish(m, h):
             if m not in ot:
                 ot[m] = tiles.tile([P, 1024], F32, name="ot")
-            sl = slice(512 * h, 512 * (h + 1))
-            nc.vector.tensor_tensor(out=ot[m][:, sl], in0=ps[(3, m, h)][:], in1=a[(1, m)][:, sl], op=ALU.add)
-            nc.sync.dma_start(out=out[128 * m : 128 * (m + 1), sl], in_=ot[m][:, sl])
+            step = 256 if (m, h) == (7, 1) else 512
+            for c in range(0, 512, step):
+                sl = slice(512 * h + c, 512 * h + c + step)
+                nc.vector.tensor_tensor(out=ot[m][:, sl], in0=ps[(3, m, h)][:, c : c + step], in1=a[(1, m)][:, sl], op=ALU.add)
+                nc.sync.dma_start(out=out[128 * m : 128 * (m + 1), sl], in_=ot[m][:, sl])
 
         with tc.manual_schedule():
+            nc.vector.memset(s1[:].rearrange("p g n -> p (g n)").bitcast(I32), 0)
             nc.vector.memset(wbf[:], 1.0)
             nc.vector.quantize_mx(out=wcd[:].bitcast(FP8X4), scales=wsc[:], in_=wbf[:])
-            nc.vector.memset(s1[:].rearrange("p g n -> p (g n)").bitcast(I32), 0)
-            nc.vector.memset(s2[:].rearrange("p g n -> p (g n)").bitcast(I32), 0)
-            nc.vector.memset(dummy[:], 0.0)
-            nc.scalar.activation(out=dummy[:], in_=dummy[:], func=ABS)
             make_identity(nc, ident[:])
-            warm = psum.tile([P, 512], F32, name="acc")
-            for i in range(12):
-                nc.tensor.matmul_mx(out=warm[:, 0:128], lhsT=wcd[:].bitcast(FP8X4), lhsT_scale=wsc[:], rhs=wcd[:].bitcast(FP8X4), rhs_scale=wsc[:], start=True, stop=True)
-            for step in ORDER.split():
+            nc.gpsimd.memset(dummy[:], 0.0)
+            nc.gpsimd.memset(s2[:].rearrange("p g n -> p (g n)").bitcast(I32), 0)
+            warm_up(12)
+            steps = ORDER.split()
+            for step in steps:
                 w = step.split("_")
                 k = w[0]
                 v = [int(c) for c in w[1:] if c in "01234567"]
                 if k == "LX":
                     load_x([int(c) for c in w[1]])
                 elif k == "LS1":
-                    load_scales(s1, w1_scales)
+                    load_scales(s1, w1_scales, nc.sync)
+                    nc.scalar.activation(out=dummy[:], in_=dummy[:], func=ABS)
                 elif k == "LS2":
-                    load_scales(s2, w2_scales)
+                    load_scales(s2, w2_scales, nc.sync)
                 elif k == "L1":
                     load_w1(w[1])
                 elif k == "L2":
@@ -186,6 +218,14 @@ def tile_coarray_cosine_spectrum_s10_kernel(tc, x, w1_words, w1_scales, w2_words
                     load_w3(w[1])
                 elif k == "T":
                     transp(v[0])
+                    if v[0] == 1:
+                        warm_up(6)
+                elif k == "XR":
+                    reorder(v[0], w[2])
+                elif k == "OG":
+                    finish_g(v[0], v[1])
+                elif k == "CP":
+                    copy_g(v[0], v[1])
                 elif k == "XC":
                     xcopy(v[0], w[2])
                 elif k == "XQ":
@@ -199,6 +239,6 @@ def tile_coarray_cosine_spectrum_s10_kernel(tc, x, w1_words, w1_scales, w2_words
                 elif k == "A":
                     absolute(v[0], v[1], v[2])
                 elif k == "M":
-                    minimum(v[0], v[1])
+                    minimum(v[0], w[2])
                 elif k == "O":
                     finish(v[0], v[1])

@@ -15,7 +15,7 @@ ABS = mybir.ActivationFunctionType.Abs
 ALU = mybir.AluOpType
 P = 128
 
-ORDER = """LX_0 LX_1 LS1 L1_a LX_23 L3_g0 LX_45 LS2 L2_a L3_g1 LX_67 T_0 T_1 XC_0_S XC_1_S XQ_0 P_1_0_0 XQ_1 P_1_0_1 A_1_0_0 A_1_0_1 T_2 T_3 XC_2_S P_1_1_0 XC_3_S XQ_2 P_1_1_1 A_1_1_0 XQ_3 WC_0_0_V P_1_2_0 A_1_1_1 P_1_2_1 A_1_2_0 WC_0_1_V T_4 A_1_2_1 T_5 XC_4_S P_1_3_0 XC_5_S XQ_4 WQ_0_0 P_1_3_1 A_1_3_0 XQ_5 P_1_4_0 A_1_3_1 WQ_0_1 P_1_4_1 A_1_4_0 P_2_0_0 A_1_4_1 WC_1_0_V P_2_0_1 A_2_0_0 P_2_1_0 A_2_0_1 P_2_1_1 A_2_1_0 WC_1_1_V T_6 A_2_1_1 T_7 XC_6_S WQ_1_0 P_1_5_0 XC_7_S WQ_1_1 P_1_5_1 A_1_5_0 M_0_f P_2_2_0 A_1_5_1 P_2_2_1 A_2_2_0 XQ_6 P_2_3_0 M_1_f A_2_2_1 P_2_3_1 A_2_3_0 M_2_f P_2_4_0 A_2_3_1 P_2_4_1 A_2_4_0 XQ_7 P_3_0_0 A_2_4_1 M_3_f P_3_0_1 P_2_5_0 O_0_0 P_2_5_1 A_2_5_0 O_0_1 P_3_1_0 A_2_5_1 M_4_f P_3_1_1 P_1_6_0 O_1_0 P_1_6_1 A_1_6_0 O_1_1 P_3_2_0 A_1_6_1 M_5_f P_3_2_1 P_2_6_0 O_2_0 P_2_6_1 A_2_6_0 O_2_1 P_3_3_0 A_2_6_1 P_3_3_1 O_3_0 P_1_7_0 O_3_1 P_1_7_1 A_1_7_0 M_6_f P_3_4_0 A_1_7_1 P_3_4_1 O_4_0 P_3_5_0 O_4_1 P_3_5_1 O_5_0 P_2_7_0 O_5_1 P_2_7_1 A_2_7_0 P_3_6_0 A_2_7_1 M_7_0 P_3_6_1 O_6_0 P_3_7_0 O_6_1 P_3_7_1 M_7_1 O_7_0 O_7_1"""
+ORDER = """LX_0 LX_1 LS1 L1_a LX_23 LX_45 L3_g0 LS2 L2_a L3_g1 LX_67 T_0 T_1 XC_0_S XC_1_S XQ_0 XQ_1 P_1_0_0 P_1_0_1 A_1_0_0 XR_2_V A_1_0_1 XR_3_V T_2 T_3 XC_2_S XR_4_V P_1_1_0 XC_3_V P_1_1_1 A_1_1_0 XQ_2 XQ_3 P_1_2_0 A_1_1_1 XR_5_V P_1_2_1 A_1_2_0 WC_0_0_V A_1_2_1 T_4 T_5 XC_4_S P_1_3_0 XC_5_S XQ_4 P_1_3_1 WQ_0_0 A_1_3_0 P_1_4_0 XQ_5 A_1_3_1 P_1_4_1 WC_0_1_V A_1_4_0 P_2_0_0 A_1_4_1 P_2_0_1 A_2_0_0 WQ_0_1 P_2_1_0 A_2_0_1 P_2_1_1 WC_1_0_V A_2_1_0 P_1_5_0 A_2_1_1 P_1_5_1 WC_1_1_V A_1_5_0 T_6 A_1_5_1 T_7 XC_6_S WQ_1_0 P_2_2_0 XC_7_S WQ_1_1 P_2_2_1 A_2_2_0 M_0_f P_2_3_0 A_2_2_1 P_2_3_1 A_2_3_0 XQ_6 P_2_4_0 M_1_f A_2_3_1 P_2_4_1 A_2_4_0 P_3_0_0 M_2_f A_2_4_1 P_3_0_1 O_0_0 P_2_5_0 O_0_1 P_2_5_1 A_2_5_0 XQ_7 P_3_1_0 A_2_5_1 M_3_f P_3_1_1 P_1_6_0 O_1_0 P_1_6_1 A_1_6_0 O_1_1 P_3_2_0 A_1_6_1 M_4_f P_3_2_1 P_2_6_0 O_2_0 P_2_6_1 A_2_6_0 O_2_1 P_3_3_0 A_2_6_1 M_5_f P_3_3_1 P_1_7_0 O_3_0 P_1_7_1 A_1_7_0 O_3_1 P_3_4_0 A_1_7_1 M_6_f P_3_4_1 P_3_5_0 O_4_0 P_3_5_1 O_4_1 P_2_7_0 O_5_0 P_2_7_1 O_5_1 A_2_7_0 P_3_6_0 A_2_7_1 M_7_0 M_7_1 P_3_6_1 O_6_0 P_3_7_0 O_6_1 P_3_7_1 O_7_0 O_7_1"""
 
 
 def tile_coarray_cosine_spectrum_s10_kernel(tc, x, w1_words, w1_scales, w2_words, w2_scales, w3, out):

from contextlib import ExitStack
import concourse.mybir as mybir
from concourse.masks import make_identity

FLOPS = 3 * 2 * 1024 * 1024 * 1024

F32 = mybir.dt.float32
BF16 = mybir.dt.bfloat16
U32 = mybir.dt.uint32
I32 = mybir.dt.int32
U8 = mybir.dt.uint8
FP8X4 = mybir.dt.float8_e4m3fn_x4
FP4X4 = mybir.dt.float4_e2m1fn_x4
ABS = mybir.ActivationFunctionType.Abs
ALU = mybir.AluOpType
P = 128

ORDER = """LX_0 LX_1 LS1 L1_a LX_23 LX_45 L3_g0 LS2 L2_a L3_g1 LX_67 T_0 T_1 XC_0_S XC_1_S XQ_0 XQ_1 P_1_0_0 P_1_0_1 A_1_0_0 XR_2_V A_1_0_1 XR_3_V T_2 T_3 XC_2_S XR_4_V P_1_1_0 XC_3_V P_1_1_1 A_1_1_0 XQ_2 XQ_3 P_1_2_0 A_1_1_1 XR_5_V P_1_2_1 A_1_2_0 WC_0_0_V A_1_2_1 T_4 T_5 XC_4_S P_1_3_0 XC_5_S XQ_4 P_1_3_1 WQ_0_0 A_1_3_0 P_1_4_0 XQ_5 A_1_3_1 P_1_4_1 WC_0_1_V A_1_4_0 P_2_0_0 A_1_4_1 P_2_0_1 A_2_0_0 WQ_0_1 P_2_1_0 A_2_0_1 P_2_1_1 WC_1_0_V A_2_1_0 P_1_5_0 A_2_1_1 P_1_5_1 WC_1_1_V A_1_5_0 T_6 A_1_5_1 T_7 XC_6_S WQ_1_0 P_2_2_0 XC_7_S WQ_1_1 P_2_2_1 A_2_2_0 M_0_f P_2_3_0 A_2_2_1 P_2_3_1 A_2_3_0 XQ_6 P_2_4_0 M_1_f A_2_3_1 P_2_4_1 A_2_4_0 P_3_0_0 M_2_f A_2_4_1 P_3_0_1 O_0_0 P_2_5_0 O_0_1 P_2_5_1 A_2_5_0 XQ_7 P_3_1_0 A_2_5_1 M_3_f P_3_1_1 P_1_6_0 O_1_0 P_1_6_1 A_1_6_0 O_1_1 P_3_2_0 A_1_6_1 M_4_f P_3_2_1 P_2_6_0 O_2_0 P_2_6_1 A_2_6_0 O_2_1 P_3_3_0 A_2_6_1 M_5_f P_3_3_1 P_1_7_0 O_3_0 P_1_7_1 A_1_7_0 O_3_1 P_3_4_0 A_1_7_1 M_6_f P_3_4_1 P_3_5_0 O_4_0 P_3_5_1 O_4_1 P_2_7_0 O_5_0 P_2_7_1 O_5_1 A_2_7_0 P_3_6_0 A_2_7_1 M_7_0 M_7_1 P_3_6_1 O_6_0 P_3_7_0 O_6_1 P_3_7_1 O_7_0 O_7_1"""


def tile_coarray_cosine_spectrum_s10_kernel(tc, x, w1_words, w1_scales, w2_words, w2_scales, w3, out):
    nc = tc.nc
    with ExitStack() as ctx:
        one = ctx.enter_context(tc.tile_pool(name="one", bufs=1))
        tiles = ctx.enter_context(tc.tile_pool(name="tiles", bufs=8))
        psum = ctx.enter_context(tc.psum_pool(name="psum", bufs=6))
        psum_t = ctx.enter_context(tc.psum_pool(name="psum_t", bufs=2))

        ident = one.tile([P, P], F32, name="ident")
        w1 = one.tile([P, 2, 2048], U8, name="w1", align_bytes=64)
        s1 = one.tile([P, 2, 1024], U8, name="s1", align_bytes=64)
        w2 = one.tile([P, 2, 4096], U8, name="w2", align_bytes=64)
        s2 = one.tile([P, 2, 1024], U8, name="s2", align_bytes=64)
        raw3 = [one.tile([P, 4, 1024], BF16, name="raw3_%d" % g, align_bytes=64) for g in range(2)]
        grp3 = [one.tile([P, 2048], BF16, name="grp3_%d" % i, align_bytes=64) for i in range(4)]
        w3c = [one.tile([P, 512], U32, name="w3c_%d" % i, align_bytes=64) for i in range(4)]
        w3s = [one.tile([P, 512], U8, name="w3s_%d" % i, align_bytes=64) for i in range(4)]
        dummy = one.tile([P, 1], F32, name="dummy")
        wbf = one.tile([P, 512], BF16, name="wbf", align_bytes=64)
        wcd = one.tile([P, 128], U32, name="wcd", align_bytes=64)
        wsc = one.tile([P, 128], U8, name="wsc", align_bytes=64)

        xr = [None] * 8
        xt = [None] * 8
        xg = [None] * 8
        xc = [None] * 8
        xs = [None] * 8
        a = {}
        xo = {}
        pc = {}
        ot = {}
        ps = {}

        def warm_up(n):
            warm = psum.tile([P, 512], F32, name="acc")
            for i in range(n):
                nc.tensor.matmul_mx(out=warm[:, 0:128], lhsT=wcd[:].bitcast(FP8X4), lhsT_scale=wsc[:], rhs=wcd[:].bitcast(FP8X4), rhs_scale=wsc[:], start=True, stop=True)

        def load_x(ms):
            if len(ms) == 1:
                t = tiles.tile([P, 1, 1024], BF16, name="xr1", align_bytes=64, bufs=2)
            else:
                t = tiles.tile([P, 2, 1024], BF16, name="xr2", align_bytes=64, bufs=3)
            for i in range(len(ms)):
                xr[ms[i]] = t[:, i, :]
            m = ms[0]
            nc.sync.dma_start(out=t[:], in_=x[128 * m : 128 * (m + len(ms)), :].rearrange("(i r) k -> r i k", r=128))

        def load_scales(s, src, eng=nc.sync):
            for q in range(4):
                eng.dma_start(
                    out=s[32 * q : 32 * q + 4, :, :].bitcast(I32),
                    in_=src[:, 4 * q : 4 * q + 4, :].rearrange("g q n -> q g n").bitcast(I32),
                )

        def load_w1(h):
            sl = slice(0, 2048) if h == "a" else slice(1024 * int(h), 1024 * (int(h) + 1))
            nc.sync.dma_start(out=w1[:, :, sl].bitcast(I32), in_=w1_words[:, :, sl].rearrange("g p b -> p g b").bitcast(I32))

        def load_w2(h):
            a0, a1 = (0, 1024) if h == "a" else (512 * int(h), 512 * (int(h) + 1))
            nc.sync.dma_start(
                out=w2[:, :, 4 * a0 : 4 * a1].bitcast(I32),
                in_=w2_words[:, :, a0:a1, :].rearrange("g p n t -> p g (n t)").bitcast(I32),
            )

        def load_w3(s):
            if s[0] == "g":
                g, sl = int(s[1]), slice(0, 1024)
            else:
                g, h = int(s[0]), int(s[1])
                sl = slice(512 * h, 512 * (h + 1))
            nc.sync.dma_start(out=raw3[g][:, :, sl], in_=w3[512 * g : 512 * (g + 1), sl].rearrange("(p j) n -> p j n", j=4))

        def transp(m):
            xt[m] = psum_t.tile([P, 2, 2, 128], F32, name="xt")
            for g in range(2):
                for u in range(2):
                    if m in xo:
                        src = xo[m][:, 256 * g + 128 * u : 256 * g + 128 * (u + 1)]
                    else:
                        src = xr[m].bitcast(F32)[:, 256 * g + u : 256 * (g + 1) : 2]
                    nc.tensor.transpose(xt[m][:, g, u, :], src, ident[:])

        def reorder(m, eng):
            t = tiles.tile([P, 512], F32, name="xo", align_bytes=64)
            o = t[:].rearrange("p (g u w) -> p g u w", g=2, u=2)
            i = xr[m].bitcast(F32).rearrange("p (g w u) -> p g u w", g=2, u=2)
            if eng == "S":
                nc.scalar.copy(out=o, in_=i)
            else:
                nc.vector.tensor_copy(out=o, in_=i)
            xo[m] = t

        def xcopy(m, eng):
            xg[m] = tiles.tile([P, 1024], BF16, name="xg", align_bytes=64)
            o = xg[m][:].bitcast(F32).rearrange("p (g r u) -> p g r u", g=2, u=2)
            i = xt[m][:].rearrange("p g u r -> p g r u")
            if eng == "S":
                nc.scalar.copy(out=o, in_=i)
            else:
                nc.vector.tensor_copy(out=o, in_=i)

        def xquant(m):
            xc[m] = tiles.tile([P, 256], U32, name="xc", align_bytes=64)
            xs[m] = tiles.tile([P, 256], U8, name="xs", align_bytes=64)
            nc.vector.quantize_mx(out=xc[m][:].bitcast(FP8X4), scales=xs[m][:], in_=xg[m][:])

        def w3copy(g, h, eng):
            o = grp3[2 * g + h][:].rearrange("p (c i t) -> p c t i", i=4, t=4)
            i = raw3[g][:, :, 512 * h : 512 * (h + 1)].rearrange("p t (c i) -> p c t i", i=4)
            if eng == "S":
                nc.scalar.copy(out=o, in_=i)
            else:
                nc.vector.tensor_copy(out=o, in_=i)

        def w3quant(g, h):
            k = 2 * g + h
            nc.vector.quantize_mx(out=w3c[k][:].bitcast(FP8X4), scales=w3s[k][:], in_=grp3[k][:])

        def product(n, m, h):
            acc = psum.tile([P, 512], F32, name="acc")
            ps[(n, m, h)] = acc
            for g in range(2):
                if n == 1:
                    rhs = w1[:, g, 1024 * h : 1024 * (h + 1)].bitcast(FP4X4)
                    rsc = s1[:, g, 512 * h : 512 * (h + 1)]
                elif n == 2:
                    rhs = w2[:, g, 2048 * h : 2048 * (h + 1)].bitcast(FP8X4)
                    rsc = s2[:, g, 512 * h : 512 * (h + 1)]
                else:
                    rhs = w3c[2 * g + h][:].bitcast(FP8X4)
                    rsc = w3s[2 * g + h][:]
                nc.tensor.matmul_mx(
                    out=acc[:],
                    lhsT=xc[m][:, 128 * g : 128 * (g + 1)].bitcast(FP8X4),
                    lhsT_scale=xs[m][:, 128 * g : 128 * (g + 1)],
                    rhs=rhs,
                    rhs_scale=rsc,
                    start=(g == 0),
                    stop=(g == 1),
                )

        def absolute(n, m, h):
            if (n, m) not in a:
                a[(n, m)] = tiles.tile([P, 1024], F32, name="a%d" % n)
            nc.scalar.activation(out=a[(n, m)][:, 512 * h : 512 * (h + 1)], in_=ps[(n, m, h)][:], func=ABS)

        def minimum(m, h):
            sl = slice(0, 1024) if h == "f" else slice(512 * int(h), 512 * (int(h) + 1))
            nc.vector.tensor_tensor(out=a[(1, m)][:, sl], in0=a[(1, m)][:, sl], in1=a[(2, m)][:, sl], op=ALU.min)

        def copy_g(m, h):
            pc[(m, h)] = tiles.tile([P, 512], F32, name="pc", bufs=4)
            nc.scalar.copy(out=pc[(m, h)][:], in_=ps[(3, m, h)][:])

        def finish_g(m, h):
            if m not in ot:
                ot[m] = tiles.tile([P, 1024], F32, name="ot")
            sl = slice(512 * h, 512 * (h + 1))
            nc.gpsimd.tensor_tensor(out=ot[m][:, sl], in0=pc[(m, h)][:], in1=a[(1, m)][:, sl], op=ALU.add)
            nc.sync.dma_start(out=out[128 * m : 128 * (m + 1), sl], in_=ot[m][:, sl])

        def finish(m, h):
            if m not in ot:
                ot[m] = tiles.tile([P, 1024], F32, name="ot")
            step = 256 if (m, h) == (7, 1) else 512
            for c in range(0, 512, step):
                sl = slice(512 * h + c, 512 * h + c + step)
                nc.vector.tensor_tensor(out=ot[m][:, sl], in0=ps[(3, m, h)][:, c : c + step], in1=a[(1, m)][:, sl], op=ALU.add)
                nc.sync.dma_start(out=out[128 * m : 128 * (m + 1), sl], in_=ot[m][:, sl])

        with tc.manual_schedule():
            nc.vector.memset(s1[:].rearrange("p g n -> p (g n)").bitcast(I32), 0)
            nc.vector.memset(wbf[:], 1.0)
            nc.vector.quantize_mx(out=wcd[:].bitcast(FP8X4), scales=wsc[:], in_=wbf[:])
            make_identity(nc, ident[:])
            nc.gpsimd.memset(dummy[:], 0.0)
            nc.gpsimd.memset(s2[:].rearrange("p g n -> p (g n)").bitcast(I32), 0)
            warm_up(12)
            steps = ORDER.split()
            for step in steps:
                w = step.split("_")
                k = w[0]
                v = [int(c) for c in w[1:] if c in "01234567"]
                if k == "LX":
                    load_x([int(c) for c in w[1]])
                elif k == "LS1":
                    load_scales(s1, w1_scales, nc.sync)
                    nc.scalar.activation(out=dummy[:], in_=dummy[:], func=ABS)
                elif k == "LS2":
                    load_scales(s2, w2_scales, nc.sync)
                elif k == "L1":
                    load_w1(w[1])
                elif k == "L2":
                    load_w2(w[1])
                elif k == "L3":
                    load_w3(w[1])
                elif k == "T":
                    transp(v[0])
                    if v[0] == 1:
                        warm_up(6)
                elif k == "XR":
                    reorder(v[0], w[2])
                elif k == "OG":
                    finish_g(v[0], v[1])
                elif k == "CP":
                    copy_g(v[0], v[1])
                elif k == "XC":
                    xcopy(v[0], w[2])
                elif k == "XQ":
                    xquant(v[0])
                elif k == "WC":
                    w3copy(v[0], v[1], w[3])
                elif k == "WQ":
                    w3quant(v[0], v[1])
                elif k == "P":
                    product(v[0], v[1], v[2])
                elif k == "A":
                    absolute(v[0], v[1], v[2])
                elif k == "M":
                    minimum(v[0], w[2])
                elif k == "O":
                    finish(v[0], v[1])
